import numpy as np
import ml_dtypes


def mxq(x, axis, fmt="e4m3"):
    dtype, down = {"e4m3": (ml_dtypes.float8_e4m3fn, 7), "e5m2": (ml_dtypes.float8_e5m2, 14)}[fmt]
    v = np.moveaxis(np.asarray(x, np.float32).astype(ml_dtypes.bfloat16).astype(np.float64), axis, -1)
    blocks = v.reshape(v.shape[:-1] + (-1, 32))
    amax = np.abs(blocks).max(-1, keepdims=True)
    byte = np.maximum(np.where(amax > 0, np.frexp(amax)[1] - 1 + 127, 0) - down, 1)
    scale = np.exp2(byte - 127.0)
    codes = (blocks / scale).astype(np.float32).astype(dtype).astype(np.float64)
    return np.moveaxis((codes * scale).reshape(v.shape), -1, axis)


WIDE = False


def mx_kscale(k):
    if not WIDE:
        return np.ones(k)
    levels = np.array([10, -10, 5, -5, 0])
    if k % 512:
        return np.exp2(np.random.permutation(np.resize(levels, k // 32))).repeat(32)
    a = np.empty((k // 512, 16))
    for p in range(k // 512):
        a[p, :8] = np.random.permutation(np.resize(levels, 8))
        for g in range(8):
            far = levels[np.abs(levels - a[p, g]) >= 10]
            a[p, g + 8] = far[np.random.randint(len(far))]
    return np.exp2(a.ravel()).repeat(32)


BF16 = ml_dtypes.bfloat16


def bf(x):
    return np.asarray(x, np.float32).astype(BF16)


def f64(x):
    return np.asarray(x).astype(np.float64)

E4M3FN = np.array([(-1.0 if i & 128 else 1.0) * ((1.0 + (i & 7) / 8.0) * 2.0 ** (((i >> 3) & 15) - 7) if i & 120 else (i & 7) * 2.0 ** -9) for i in range(256)])


def e4m3fn_bytes(y):
    return np.clip(np.asarray(y, np.float64), -448.0, 448.0).astype(np.float32).astype(ml_dtypes.float8_e4m3fn).view(np.uint8)


def e4m3fn_values(b):
    return E4M3FN[b]

def planes(Y):
    n, m = Y.shape
    b = f64(bf(Y)).reshape(n // 32, 32, m)
    amax = np.abs(b).max(1)
    byte = np.clip(np.where(amax > 0, np.frexp(amax)[1] - 1 + 127 - 7, 1), 1, 254)
    codes = (b * np.exp2(127.0 - byte)[:, None, :]).reshape(n, m).astype(np.float32).astype(ml_dtypes.float8_e4m3fn).view(np.uint8)
    words = codes.reshape(n // 512, 128, 4, m).transpose(0, 1, 3, 2)
    return np.ascontiguousarray(words), np.ascontiguousarray(byte.astype(np.uint8).reshape(n // 512, 16, m))


S, K = 2048, 1536

SELF = 0.2
MEAN = 1.0
MIXED = 0.4


def setup_inputs():
    s = mx_kscale(K)
    site = np.exp(0.25 * np.random.randn(S, 1))
    X = site * np.exp(0.5 * np.random.randn(S, K)) * s[None, :]
    X_scale = (np.max(np.abs(X), axis=0, keepdims=True) / 448.0).astype(np.float32)
    X_bytes = e4m3fn_bytes(X / np.repeat(f64(X_scale), S, axis=0))
    A = MIXED * np.random.randn(K, K) / np.sqrt(K) + MEAN / K + SELF * np.eye(K)
    A = A / s[:, None]
    r = 1.0 + 0.3 * np.random.randn(1, K)
    gain = np.exp(0.8 * np.random.randn(1, K)) / s[None, :]
    return {"X_bytes": X_bytes, "X_scale": X_scale, "A": bf(A), "r": bf(r), "gain": bf(gain)}


def reference(X_bytes, X_scale, A, r, gain):
    X = e4m3fn_values(X_bytes) * np.repeat(f64(X_scale), S, axis=0)
    pressure = mxq(X, 1, "e4m3") @ mxq(f64(A), 0, "e4m3")
    y = (X * f64(gain)) * np.exp(f64(r) - pressure)
    Y = y.T
    words, scales = planes(Y)
    return y, words, scales

@@ -1,0 +1,354 @@
+from contextlib import ExitStack
+
+import concourse.mybir as mybir
+from concourse.masks import make_identity
+
+S, K = 2048, 1536
+FLOPS = 2 * S * K * K
+
+F32 = mybir.dt.float32
+BF16 = mybir.dt.bfloat16
+I32 = mybir.dt.int32
+U32 = mybir.dt.uint32
+U8 = mybir.dt.uint8
+FP8 = mybir.dt.float8_e4m3fn
+FP8X4 = mybir.dt.float8_e4m3fn_x4
+ALU = mybir.AluOpType
+ACT = mybir.ActivationFunctionType
+
+P = 128
+PACK = 4
+GROUP = P * PACK
+GROUPS = K // GROUP
+CHUNK = 256
+HALVES = CHUNK // P
+CHUNKS = S // CHUNK
+STEPS = CHUNKS * GROUPS
+PIECE = HALVES * K // GROUPS
+SCALAR_SITES = 0
+GPSIMD_SITES = 256
+Y_BUFS = 1
+TAIL = 20
+TAIL2 = 22
+VECTOR_WIDEN = 384
+VECTOR_PLANES = ((0, 0, 4), (4, 4, 0), (0, 0, 4))
+
+
+def tile_ricker_map_season_step_b5_kernel(tc, X_bytes, X_scale, A, r, gain, out_0, out_1, out_2):
+    nc = tc.nc
+    words_out = out_1.rearrange("g p m t -> g p (m t)").bitcast(I32)
+    scales_out = out_2.bitcast(I32)
+
+    with ExitStack() as ctx:
+        keep = ctx.enter_context(tc.tile_pool(name="keep", bufs=1))
+        work = ctx.enter_context(tc.tile_pool(name="work", bufs=2))
+        psum_x = ctx.enter_context(tc.psum_pool(name="psum_x", bufs=5))
+        psum_s = ctx.enter_context(tc.psum_pool(name="psum_s", bufs=3))
+        ctx.enter_context(tc.manual_schedule())
+
+        ident = keep.tile([P, P], F32, name="ident")
+        make_identity(nc, ident[:])
+        warm = keep.tile([P, 1], F32, name="warm")
+        nc.scalar.activation(out=warm[:], in_=ident[:, 0:1], func=ACT.Exp)
+
+        x_scale = keep.tile([P, GROUPS * PACK], F32, name="x_scale")
+        r_bf = keep.tile([P, GROUPS * PACK], BF16, name="r_bf")
+        gain_bf = keep.tile([P, GROUPS * PACK], BF16, name="gain_bf")
+        rate = keep.tile([P, GROUPS * PACK], F32, name="rate")
+        factor = keep.tile([P, GROUPS * PACK], F32, name="factor")
+
+        x_bytes = [keep.tile([P, HALVES * K], U8, name="x_bytes_%d" % i) for i in range(CHUNKS)]
+        a_raw = {}
+        a_codes = {}
+        a_scales = {}
+        for gn in range(GROUPS):
+            for gk in range(GROUPS):
+                a_raw[gk, gn] = keep.tile([P, PACK * GROUP], BF16, name="a_raw_%d_%d" % (gk, gn))
+                a_codes[gk, gn] = keep.tile([P, GROUP], U32, name="a_codes_%d_%d" % (gk, gn), align_bytes=64)
+                a_scales[gk, gn] = keep.tile([P, GROUP], U8, name="a_scales_%d_%d" % (gk, gn), align_bytes=64)
+        y_scales = [keep.tile([P, S], U8, name="y_scales_%d" % g, align_bytes=64) for g in range(GROUPS)]
+
+        def load_species_vector(dst, src):
+            nc.sync.dma_start(
+                out=dst[:].rearrange("p (g t) -> p g t", t=PACK),
+                in_=src.rearrange("o (g p t) -> p (o g) t", p=P, t=PACK),
+            )
+
+        def load_x(i):
+            nc.sync.dma_start(
+                out=x_bytes[i][:].rearrange("p (h k) -> p h k", h=HALVES),
+                in_=X_bytes[i * CHUNK : (i + 1) * CHUNK, :].rearrange("(h p) k -> p h k", p=P),
+            )
+
+        def load_a(gk, gn):
+            nc.sync.dma_start(
+                out=a_raw[gk, gn][:].rearrange("p (j c) -> p j c", j=PACK),
+                in_=A[gk * GROUP : (gk + 1) * GROUP, gn * GROUP : (gn + 1) * GROUP].rearrange("(p j) c -> p j c", j=PACK),
+            )
+
+        load_x(0)
+        load_species_vector(x_scale, X_scale)
+        for gk in range(GROUPS):
+            load_a(gk, 0)
+        load_x(1)
+        load_species_vector(r_bf, r)
+        load_species_vector(gain_bf, gain)
+        for gn in range(1, GROUPS):
+            for gk in range(GROUPS):
+                load_a(gk, gn)
+        for i in range(2, CHUNKS):
+            load_x(i)
+
+        nc.gpsimd.tensor_copy(out=rate[:], in_=r_bf[:])
+        nc.gpsimd.tensor_tensor(out=factor[:], in0=x_scale[:], in1=gain_bf[:], op=ALU.mult)
+
+        x_wide = {}
+        x_turned = {}
+        x_grouped = {}
+        x_codes = {}
+        x_scales = {}
+        pressure = {}
+        growth = {}
+        y_planes = {}
+        y_grouped = {}
+        y_turned = {}
+        a_grouped = {}
+        y_rows = {}
+
+        def widen(m, cut):
+            i, j = divmod(m, GROUPS)
+            if j == 0:
+                x_wide[i] = work.tile([P, HALVES * K], BF16, name="x_wide")
+            first = j * PIECE
+            for copy, cols in (
+                (nc.scalar.copy, slice(first + cut, first + PIECE)),
+                (nc.vector.tensor_copy, slice(first, first + cut)),
+            ):
+                if cols.stop > cols.start:
+                    copy(out=x_wide[i][:, cols], in_=x_bytes[i][:, cols].bitcast(FP8))
+
+        def turn_x(n):
+            i, g = divmod(n, GROUPS)
+            x_turned[n] = psum_x.tile([P, 2, CHUNK], F32, name="x_turned")
+            words = x_wide[i][:].bitcast(F32)
+            for h in range(HALVES):
+                first = (h * K + g * GROUP) // 2
+                for u in range(2):
+                    nc.tensor.transpose(
+                        x_turned[n][:, u, h * P : (h + 1) * P], words[:, first + u : first + 2 * P : 2], ident[:]
+                    )
+
+        def raw_view(n):
+            return x_turned[n][:].rearrange("p u s -> p (u s)").bitcast(BF16).rearrange("p (u s e) -> p s u e", u=2, e=2)
+
+        def scale_x(n):
+            g = n % GROUPS
+            x_grouped[n] = work.tile([P, CHUNK * PACK], BF16, name="x_grouped", align_bytes=64)
+            nc.vector.tensor_tensor(
+                out=x_grouped[n][:].rearrange("p (s u e) -> p s u e", u=2, e=2),
+                in0=raw_view(n),
+                in1=x_scale[:, g * PACK : (g + 1) * PACK]
+                .rearrange("p (u e) -> p u e", u=2)
+                .unsqueeze(1)
+                .to_broadcast([P, CHUNK, 2, 2]),
+                op=ALU.mult,
+            )
+
+        def quantize_x(n):
+            x_codes[n] = work.tile([P, CHUNK], U32, name="x_codes", bufs=2 * GROUPS, align_bytes=64)
+            x_scales[n] = work.tile([P, CHUNK], U8, name="x_scales", bufs=2 * GROUPS, align_bytes=64)
+            nc.vector.quantize_mx(out=x_codes[n][:].bitcast(FP8X4), scales=x_scales[n][:], in_=x_grouped[n][:])
+
+        def group_a(gk, gn):
+            a_grouped[gk, gn] = work.tile([P, GROUP * PACK], BF16, name="a_grouped", bufs=4, align_bytes=64)
+            src = a_raw[gk, gn][:].rearrange("p (j m t) -> p m t j", j=PACK, t=PACK)
+            dst = a_grouped[gk, gn][:].rearrange("p (t m j) -> p m t j", t=PACK, j=PACK)
+            cut = VECTOR_PLANES[gn][gk]
+            if cut < PACK:
+                nc.scalar.copy(out=dst[:, :, cut:, :], in_=src[:, :, cut:, :])
+            if cut > 0:
+                nc.vector.tensor_copy(out=dst[:, :, :cut, :], in_=src[:, :, :cut, :])
+
+        def quantize_a(gk, gn):
+            nc.vector.quantize_mx(out=a_codes[gk, gn][:].bitcast(FP8X4), scales=a_scales[gk, gn][:], in_=a_grouped[gk, gn][:])
+
+        def multiply(n, halves):
+            i, gn = divmod(n, GROUPS)
+            for u in halves:
+                pressure[n, u] = psum_s.tile([P, 2, CHUNK], F32, name="pressure", tag="bank")
+                for e in range(2):
+                    cols = slice((2 * u + e) * P, (2 * u + e + 1) * P)
+                    for gk in range(GROUPS):
+                        nc.tensor.matmul_mx(
+                            out=pressure[n, u][:, e, :],
+                            lhsT=a_codes[gk, gn][:, cols].bitcast(FP8X4),
+                            lhsT_scale=a_scales[gk, gn][:, cols],
+                            rhs=x_codes[i * GROUPS + gk][:].bitcast(FP8X4),
+                            rhs_scale=x_scales[i * GROUPS + gk][:],
+                            start=(gk == 0),
+                            stop=(gk == GROUPS - 1),
+                        )
+
+        def exponentiate(n, u):
+            g = n % GROUPS
+            for t in (2 * u, 2 * u + 1):
+                growth[n, t] = work.tile([P, CHUNK], F32, name="growth", bufs=3 * PACK)
+                col = g * PACK + t
+                nc.scalar.activation(
+                    out=growth[n, t][:],
+                    in_=pressure[n, t // 2][:, t % 2, :],
+                    func=ACT.Exp,
+                    bias=rate[:, col : col + 1],
+                    scale=-1.0,
+                )
+
+        def grow(n):
+            g = n % GROUPS
+            y_planes[n] = work.tile([P, PACK * CHUNK], F32, name="y_planes", bufs=3)
+            raw = raw_view(n)
+            for t in range(PACK):
+                col = g * PACK + t
+                nc.vector.scalar_tensor_tensor(
+                    out=y_planes[n][:, t * CHUNK : (t + 1) * CHUNK],
+                    in0=raw[:, :, t // 2, t % 2],
+                    scalar=factor[:, col : col + 1],
+                    in1=growth[n, t][:],
+                    op0=ALU.mult,
+                    op1=ALU.mult,
+                )
+
+        def group_y(n):
+            y_grouped[n] = work.tile([P, CHUNK * PACK], BF16, name="y_grouped", bufs=Y_BUFS, align_bytes=64)
+            src = y_planes[n][:].rearrange("p (t c i) -> p c t i", t=PACK, i=4)
+            dst = y_grouped[n][:].rearrange("p (c i t) -> p c t i", t=PACK, i=4)
+            cut = SCALAR_SITES // 4
+            cut2 = cut + GPSIMD_SITES // 4
+            if n >= TAIL2:
+                cut, cut2 = 0, 0
+            if cut:
+                nc.scalar.copy(out=dst[:, :cut], in_=src[:, :cut])
+            if cut2 > cut:
+                nc.gpsimd.tensor_scalar(
+                    out=y_grouped[n][:].rearrange("p (s t) -> p s t", t=PACK)[:, 4 * cut : 4 * cut2],
+                    in0=y_planes[n][:].rearrange("p (t s) -> p s t", t=PACK)[:, 4 * cut : 4 * cut2],
+                    scalar1=1.0,
+                    scalar2=1.0,
+                    op0=ALU.mult,
+                    op1=ALU.mult,
+                )
+            if cut2 < CHUNK // 4:
+                nc.vector.tensor_copy(out=dst[:, cut2:], in_=src[:, cut2:])
+
+        def quantize_y(n):
+            i, g = divmod(n, GROUPS)
+            sites = slice(i * CHUNK, (i + 1) * CHUNK)
+            y_codes = work.tile([P, CHUNK], U32, name="y_codes", bufs=4, align_bytes=64)
+            nc.vector.quantize_mx(out=y_codes[:].bitcast(FP8X4), scales=y_scales[g][:, sites], in_=y_grouped[n][:])
+            nc.sync.dma_start(out=words_out[g][:, sites], in_=y_codes[:].bitcast(I32))
+            if (i + 1) % (CHUNKS // 2) == 0:
+                cols = slice((i + 1) * CHUNK // 4 - S // 8, (i + 1) * CHUNK // 4)
+                for q in range(4):
+                    nc.sync.dma_start(
+                        out=scales_out[g][4 * q : 4 * q + 4, cols],
+                        in_=y_scales[g][:].bitcast(I32)[32 * q : 32 * q + 4, cols],
+                    )
+
+        def turn_y(n, h):
+            if True:
+                y_turned[n, h] = psum_s.tile([P, PACK, P], F32, name="y_turned", tag="bank")
+                for t in range(PACK):
+                    first = t * CHUNK + h * P
+                    nc.tensor.transpose(y_turned[n, h][:, t, :], y_planes[n][:, first : first + P], ident[:])
+
+        def copy_y(n, h):
+            copy = nc.vector.tensor_copy if h == 1 and n >= TAIL else nc.scalar.copy
+            if h == 0:
+                y_rows[n] = work.tile([P, HALVES, GROUP], F32, name="y_rows", bufs=3)
+            copy(
+                out=y_rows[n][:, h, :].rearrange("s (p t) -> s p t", t=PACK),
+                in_=y_turned[n, h][:].rearrange("s t p -> s p t"),
+            )
+
+        def store_y(n, halves):
+            i, g = divmod(n, GROUPS)
+            rows = out_0[i * CHUNK : (i + 1) * CHUNK, g * GROUP : (g + 1) * GROUP].rearrange("(h s) c -> s h c", s=P)
+            nc.sync.dma_start(out=rows[:, halves, :], in_=y_rows[n][:, halves, :])
+
+        def live(n):
+            return 0 <= n < STEPS
+
+        widen(0, PIECE)
+        widen(1, 0)
+        widen(2, PIECE)
+        for n in range(GROUPS):
+            turn_x(n)
+        group_a(0, 0)
+        scale_x(0)
+        scale_x(1)
+        quantize_x(0)
+        group_a(1, 0)
+        scale_x(2)
+        quantize_x(1)
+        group_a(2, 0)
+        quantize_a(0, 0)
+        quantize_x(2)
+        quantize_a(1, 0)
+        quantize_a(2, 0)
+        widen(3, 0)
+        widen(4, 0)
+        widen(5, 0)
+        multiply(0, (0, 1))
+        turn_x(3)
+        for gk in range(GROUPS):
+            group_a(gk, 1)
+        exponentiate(0, 0)
+        exponentiate(0, 1)
+        quantize_a(0, 1)
+        quantize_a(1, 1)
+        scale_x(3)
+        quantize_a(2, 1)
+        for n in range(0, STEPS):
+            a_blocks = [(0, 2)] if n == 0 else [(1, 2), (2, 2)] if n == 1 else []
+            if live(n + 4):
+                turn_x(n + 4)
+            if live(n - 1):
+                turn_y(n - 1, 0)
+                turn_y(n - 1, 1)
+            if live(n - 2):
+                quantize_y(n - 2)
+            if live(n + 6):
+                widen(n + 6, VECTOR_WIDEN)
+            if live(n + 3):
+                quantize_x(n + 3)
+            if live(n - 1):
+                group_y(n - 1)
+            for gk, gn in a_blocks:
+                group_a(gk, gn)
+            if live(n - 1):
+                copy_y(n - 1, 0)
+            if n == 1:
+                for gk in (0, 2, 1):
+                    quantize_a(gk, 2)
+            if live(n + 1):
+                multiply(n + 1, (0,))
+            if live(n - 1):
+                copy_y(n - 1, 1)
+                store_y(n - 1, slice(0, 2))
+            if live(n + 1):
+                multiply(n + 1, (1,))
+                exponentiate(n + 1, 0)
+                exponentiate(n + 1, 1)
+            if live(n):
+                grow(n)
+            if live(n + 4):
+                scale_x(n + 4)
+        last = STEPS - 1
+        turn_y(last, 0)
+        turn_y(last, 1)
+        quantize_y(last - 1)
+        group_y(last)
+        copy_y(last, 0)
+        store_y(last, slice(0, 1))
+        copy_y(last, 1)
+        store_y(last, slice(1, 2))
+        quantize_y(last)

@@ -28,8 +28,10 @@ PIECE = HALVES * K // GROUPS
 SCALAR_SITES = 0
 GPSIMD_SITES = 256
 Y_BUFS = 1
-TAIL = 20
+HEAD_WIDEN = 0
+TAIL = ()
 TAIL2 = 22
+LANE = 99
 VECTOR_WIDEN = 384
 VECTOR_PLANES = ((0, 0, 4), (4, 4, 0), (0, 0, 4))
 
@@ -66,7 +68,9 @@ def tile_ricker_map_season_step_b5_kernel(tc, X_bytes, X_scale, A, r, gain, out_
                 a_raw[gk, gn] = keep.tile([P, PACK * GROUP], BF16, name="a_raw_%d_%d" % (gk, gn))
                 a_codes[gk, gn] = keep.tile([P, GROUP], U32, name="a_codes_%d_%d" % (gk, gn), align_bytes=64)
                 a_scales[gk, gn] = keep.tile([P, GROUP], U8, name="a_scales_%d_%d" % (gk, gn), align_bytes=64)
-        y_scales = [keep.tile([P, S], U8, name="y_scales_%d" % g, align_bytes=64) for g in range(GROUPS)]
+        y_scales_first = keep.tile([P, S], U8, name="y_scales_first", align_bytes=64)
+        y_scales_rest = keep.tile([P, S], U8, name="y_scales_rest", align_bytes=64)
+        y_scale_rows = [y_scales_first[:], y_scales_rest[:], y_scales_rest[4:P, :]]
 
         def load_species_vector(dst, src):
             nc.sync.dma_start(
@@ -99,8 +103,6 @@ def tile_ricker_map_season_step_b5_kernel(tc, X_bytes, X_scale, A, r, gain, out_
         for i in range(2, CHUNKS):
             load_x(i)
 
-        nc.gpsimd.tensor_copy(out=rate[:], in_=r_bf[:])
-        nc.gpsimd.tensor_tensor(out=factor[:], in0=x_scale[:], in1=gain_bf[:], op=ALU.mult)
 
         x_wide = {}
         x_turned = {}
@@ -143,7 +145,7 @@ def tile_ricker_map_season_step_b5_kernel(tc, X_bytes, X_scale, A, r, gain, out_
 
         def scale_x(n):
             g = n % GROUPS
-            x_grouped[n] = work.tile([P, CHUNK * PACK], BF16, name="x_grouped", align_bytes=64)
+            x_grouped[n] = work.tile([P, CHUNK * PACK], BF16, name="x_grouped", bufs=3, align_bytes=64)
             nc.vector.tensor_tensor(
                 out=x_grouped[n][:].rearrange("p (s u e) -> p s u e", u=2, e=2),
                 in0=raw_view(n),
@@ -159,15 +161,19 @@ def tile_ricker_map_season_step_b5_kernel(tc, X_bytes, X_scale, A, r, gain, out_
             x_scales[n] = work.tile([P, CHUNK], U8, name="x_scales", bufs=2 * GROUPS, align_bytes=64)
             nc.vector.quantize_mx(out=x_codes[n][:].bitcast(FP8X4), scales=x_scales[n][:], in_=x_grouped[n][:])
 
-        def group_a(gk, gn):
-            a_grouped[gk, gn] = work.tile([P, GROUP * PACK], BF16, name="a_grouped", bufs=4, align_bytes=64)
+        def group_a(gk, gn, engine, lane):
+            a_grouped[gk, gn] = work.tile([P, GROUP * PACK], BF16, name="a_grouped_%d" % lane, bufs=1, align_bytes=64)
             src = a_raw[gk, gn][:].rearrange("p (j m t) -> p m t j", j=PACK, t=PACK)
             dst = a_grouped[gk, gn][:].rearrange("p (t m j) -> p m t j", t=PACK, j=PACK)
-            cut = VECTOR_PLANES[gn][gk]
-            if cut < PACK:
-                nc.scalar.copy(out=dst[:, :, cut:, :], in_=src[:, :, cut:, :])
-            if cut > 0:
-                nc.vector.tensor_copy(out=dst[:, :, :cut, :], in_=src[:, :, :cut, :])
+            if engine == "G":
+                nc.gpsimd.tensor_scalar(out=dst.rearrange("p m t j -> p t m j"), in0=src.rearrange("p m t j -> p t m j"), scalar1=1.0, scalar2=1.0, op0=ALU.mult, op1=ALU.mult)
+            elif engine == "S":
+                nc.scalar.copy(out=dst, in_=src)
+            elif engine == "V":
+                nc.vector.tensor_copy(out=dst, in_=src)
+            else:
+                nc.scalar.copy(out=dst[:, :, 2:, :], in_=src[:, :, 2:, :])
+                nc.vector.tensor_copy(out=dst[:, :, :2, :], in_=src[:, :, :2, :])
 
         def quantize_a(gk, gn):
             nc.vector.quantize_mx(out=a_codes[gk, gn][:].bitcast(FP8X4), scales=a_scales[gk, gn][:], in_=a_grouped[gk, gn][:])
@@ -218,7 +224,7 @@ def tile_ricker_map_season_step_b5_kernel(tc, X_bytes, X_scale, A, r, gain, out_
                 )
 
         def group_y(n):
-            y_grouped[n] = work.tile([P, CHUNK * PACK], BF16, name="y_grouped", bufs=Y_BUFS, align_bytes=64)
+            y_grouped[n] = work.tile([P, CHUNK * PACK], BF16, name="y_grouped", tag="a_grouped_%d" % (0 if n == LANE else 1), bufs=1, align_bytes=64)
             src = y_planes[n][:].rearrange("p (t c i) -> p c t i", t=PACK, i=4)
             dst = y_grouped[n][:].rearrange("p (c i t) -> p c t i", t=PACK, i=4)
             cut = SCALAR_SITES // 4
@@ -243,25 +249,31 @@ def tile_ricker_map_season_step_b5_kernel(tc, X_bytes, X_scale, A, r, gain, out_
             i, g = divmod(n, GROUPS)
             sites = slice(i * CHUNK, (i + 1) * CHUNK)
             y_codes = work.tile([P, CHUNK], U32, name="y_codes", bufs=4, align_bytes=64)
-            nc.vector.quantize_mx(out=y_codes[:].bitcast(FP8X4), scales=y_scales[g][:, sites], in_=y_grouped[n][:])
+            nc.vector.quantize_mx(out=y_codes[:].bitcast(FP8X4), scales=y_scale_rows[g][:, sites], in_=y_grouped[n][:])
             nc.sync.dma_start(out=words_out[g][:, sites], in_=y_codes[:].bitcast(I32))
-            if (i + 1) % (CHUNKS // 2) == 0:
+            if (i + 1) % (CHUNKS // 2) == 0 and g != 1:
                 cols = slice((i + 1) * CHUNK // 4 - S // 8, (i + 1) * CHUNK // 4)
+                groups = slice(0, 1) if g == 0 else slice(1, GROUPS)
+                rows = 4 * (groups.stop - groups.start)
+                tile = y_scales_first if g == 0 else y_scales_rest
                 for q in range(4):
                     nc.sync.dma_start(
-                        out=scales_out[g][4 * q : 4 * q + 4, cols],
-                        in_=y_scales[g][:].bitcast(I32)[32 * q : 32 * q + 4, cols],
+                        out=scales_out[groups, 4 * q : 4 * q + 4, cols],
+                        in_=tile[:].bitcast(I32)[32 * q : 32 * q + rows, cols],
                     )
 
         def turn_y(n, h):
-            if True:
+            if h == 0 and n >= STEPS - 5:
+                y_turned[n, h] = psum_x.tile([P, PACK, P], F32, name="y_turned", tag="x_turned")
+            else:
                 y_turned[n, h] = psum_s.tile([P, PACK, P], F32, name="y_turned", tag="bank")
+            if True:
                 for t in range(PACK):
                     first = t * CHUNK + h * P
                     nc.tensor.transpose(y_turned[n, h][:, t, :], y_planes[n][:, first : first + P], ident[:])
 
         def copy_y(n, h):
-            copy = nc.vector.tensor_copy if h == 1 and n >= TAIL else nc.scalar.copy
+            copy = nc.vector.tensor_copy if h == 1 and n in TAIL else nc.scalar.copy
             if h == 0:
                 y_rows[n] = work.tile([P, HALVES, GROUP], F32, name="y_rows", bufs=3)
             copy(
@@ -282,33 +294,59 @@ def tile_ricker_map_season_step_b5_kernel(tc, X_bytes, X_scale, A, r, gain, out_
         widen(2, PIECE)
         for n in range(GROUPS):
             turn_x(n)
-        group_a(0, 0)
-        scale_x(0)
-        scale_x(1)
-        quantize_x(0)
-        group_a(1, 0)
-        scale_x(2)
-        quantize_x(1)
-        group_a(2, 0)
-        quantize_a(0, 0)
-        quantize_x(2)
-        quantize_a(1, 0)
-        quantize_a(2, 0)
-        widen(3, 0)
-        widen(4, 0)
-        widen(5, 0)
+        group_a(0, 0, "S", 0)
+        group_a(1, 0, "G", 1)
+        group_a(2, 0, "S", 2)
+        for n in range(GROUPS):
+            scale_x(n)
+        nc.vector.tensor_copy(out=rate[:], in_=r_bf[:])
+        nc.vector.tensor_tensor(out=factor[:], in0=x_scale[:], in1=gain_bf[:], op=ALU.mult)
+        for n in range(GROUPS):
+            quantize_x(n)
+            quantize_a(n, 0)
+        widen(3, HEAD_WIDEN)
+        widen(4, HEAD_WIDEN)
+        widen(5, HEAD_WIDEN)
         multiply(0, (0, 1))
         turn_x(3)
-        for gk in range(GROUPS):
-            group_a(gk, 1)
+        turn_x(4)
+        group_a(0, 1, "V", 0)
         exponentiate(0, 0)
         exponentiate(0, 1)
+        group_a(2, 1, "S", 1)
         quantize_a(0, 1)
-        quantize_a(1, 1)
+        group_a(1, 1, "G", 0)
         scale_x(3)
+        grow(0)
+        scale_x(4)
+        turn_y(0, 0)
+        turn_y(0, 1)
+        turn_x(5)
+        quantize_a(1, 1)
         quantize_a(2, 1)
-        for n in range(0, STEPS):
-            a_blocks = [(0, 2)] if n == 0 else [(1, 2), (2, 2)] if n == 1 else []
+        copy_y(0, 0)
+        copy_y(0, 1)
+        store_y(0, slice(0, 2))
+        multiply(1, (0, 1))
+        group_a(1, 2, "S", 2)
+        quantize_x(3)
+        group_a(0, 2, "V", 0)
+        quantize_x(4)
+        group_a(2, 2, "V", 1)
+        exponentiate(1, 0)
+        exponentiate(1, 1)
+        quantize_a(0, 2)
+        quantize_a(1, 2)
+        quantize_a(2, 2)
+        widen(6, 0)
+        widen(7, 0)
+        multiply(2, (0, 1))
+        group_y(0)
+        grow(1)
+        scale_x(5)
+        exponentiate(2, 0)
+        exponentiate(2, 1)
+        for n in range(2, TAIL2 + 1):
             if live(n + 4):
                 turn_x(n + 4)
             if live(n - 1):
@@ -322,13 +360,8 @@ def tile_ricker_map_season_step_b5_kernel(tc, X_bytes, X_scale, A, r, gain, out_
                 quantize_x(n + 3)
             if live(n - 1):
                 group_y(n - 1)
-            for gk, gn in a_blocks:
-                group_a(gk, gn)
             if live(n - 1):
                 copy_y(n - 1, 0)
-            if n == 1:
-                for gk in (0, 2, 1):
-                    quantize_a(gk, 2)
             if live(n + 1):
                 multiply(n + 1, (0,))
             if live(n - 1):
@@ -342,13 +375,22 @@ def tile_ricker_map_season_step_b5_kernel(tc, X_bytes, X_scale, A, r, gain, out_
                 grow(n)
             if live(n + 4):
                 scale_x(n + 4)
-        last = STEPS - 1
-        turn_y(last, 0)
-        turn_y(last, 1)
-        quantize_y(last - 1)
-        group_y(last)
-        copy_y(last, 0)
-        store_y(last, slice(0, 1))
-        copy_y(last, 1)
-        store_y(last, slice(1, 2))
-        quantize_y(last)
+        quantize_y(TAIL2 - 1)
+        for n in range(TAIL2 + 1, STEPS + 1):
+            turn_y(n - 1, 0)
+            turn_y(n - 1, 1)
+            group_y(n - 1)
+            copy_y(n - 1, 0)
+            if live(n + 1):
+                multiply(n + 1, (0,))
+            if n == STEPS:
+                store_y(n - 1, slice(0, 1))
+            copy_y(n - 1, 1)
+            store_y(n - 1, slice(1 if n == STEPS else 0, 2))
+            if live(n + 1):
+                multiply(n + 1, (1,))
+                exponentiate(n + 1, 0)
+                exponentiate(n + 1, 1)
+            if live(n):
+                grow(n)
+            quantize_y(n - 1)

@@ -30,9 +30,9 @@ GPSIMD_SITES = 256
 Y_BUFS = 1
 HEAD_WIDEN = 0
 TAIL = ()
-TAIL2 = 22
-LANE = 99
-VECTOR_WIDEN = 384
+TAIL2 = 23
+LANE = 23
+VECTOR_WIDEN = 0
 VECTOR_PLANES = ((0, 0, 4), (4, 4, 0), (0, 0, 4))
 
 
@@ -311,9 +311,9 @@ def tile_ricker_map_season_step_b5_kernel(tc, X_bytes, X_scale, A, r, gain, out_
         turn_x(3)
         turn_x(4)
         group_a(0, 1, "V", 0)
+        group_a(2, 1, "S", 1)
         exponentiate(0, 0)
         exponentiate(0, 1)
-        group_a(2, 1, "S", 1)
         quantize_a(0, 1)
         group_a(1, 1, "G", 0)
         scale_x(3)
@@ -324,15 +324,16 @@ def tile_ricker_map_season_step_b5_kernel(tc, X_bytes, X_scale, A, r, gain, out_
         turn_x(5)
         quantize_a(1, 1)
         quantize_a(2, 1)
+        group_a(1, 2, "S", 2)
         copy_y(0, 0)
+        multiply(1, (0,))
         copy_y(0, 1)
         store_y(0, slice(0, 2))
-        multiply(1, (0, 1))
-        group_a(1, 2, "S", 2)
+        multiply(1, (1,))
         quantize_x(3)
         group_a(0, 2, "V", 0)
         quantize_x(4)
-        group_a(2, 2, "V", 1)
+        group_a(2, 2, "VS", 1)
         exponentiate(1, 0)
         exponentiate(1, 1)
         quantize_a(0, 2)
@@ -346,7 +347,7 @@ def tile_ricker_map_season_step_b5_kernel(tc, X_bytes, X_scale, A, r, gain, out_
         scale_x(5)
         exponentiate(2, 0)
         exponentiate(2, 1)
-        for n in range(2, TAIL2 + 1):
+        for n in range(2, STEPS):
             if live(n + 4):
                 turn_x(n + 4)
             if live(n - 1):
@@ -375,22 +376,12 @@ def tile_ricker_map_season_step_b5_kernel(tc, X_bytes, X_scale, A, r, gain, out_
                 grow(n)
             if live(n + 4):
                 scale_x(n + 4)
-        quantize_y(TAIL2 - 1)
-        for n in range(TAIL2 + 1, STEPS + 1):
-            turn_y(n - 1, 0)
-            turn_y(n - 1, 1)
-            group_y(n - 1)
-            copy_y(n - 1, 0)
-            if live(n + 1):
-                multiply(n + 1, (0,))
-            if n == STEPS:
-                store_y(n - 1, slice(0, 1))
-            copy_y(n - 1, 1)
-            store_y(n - 1, slice(1 if n == STEPS else 0, 2))
-            if live(n + 1):
-                multiply(n + 1, (1,))
-                exponentiate(n + 1, 0)
-                exponentiate(n + 1, 1)
-            if live(n):
-                grow(n)
-            quantize_y(n - 1)
+        last = STEPS - 1
+        turn_y(last, 0)
+        turn_y(last, 1)
+        group_y(last)
+        quantize_y(last - 1)
+        copy_y(last, 0)
+        copy_y(last, 1)
+        store_y(last, slice(0, 2))
+        quantize_y(last)

@@ -104,6 +104,9 @@ def tile_ricker_map_season_step_b5_kernel(tc, X_bytes, X_scale, A, r, gain, out_
             load_x(i)
 
 
+        ones = keep.tile([P, 1], F32, name="ones")
+        nc.vector.memset(ones[:], 1.0)
+        sorted_blocks = set()
         x_wide = {}
         x_turned = {}
         x_grouped = {}
@@ -117,28 +120,37 @@ def tile_ricker_map_season_step_b5_kernel(tc, X_bytes, X_scale, A, r, gain, out_
         a_grouped = {}
         y_rows = {}
 
-        def widen(m, cut):
+        def widen(m, vector_blocks):
             i, j = divmod(m, GROUPS)
             if j == 0:
                 x_wide[i] = work.tile([P, HALVES * K], BF16, name="x_wide")
             first = j * PIECE
-            for copy, cols in (
-                (nc.scalar.copy, slice(first + cut, first + PIECE)),
-                (nc.vector.tensor_copy, slice(first, first + cut)),
-            ):
-                if cols.stop > cols.start:
-                    copy(out=x_wide[i][:, cols], in_=x_bytes[i][:, cols].bitcast(FP8))
+            cut = first + vector_blocks * GROUP
+            if cut < first + PIECE:
+                nc.scalar.copy(out=x_wide[i][:, cut : first + PIECE], in_=x_bytes[i][:, cut : first + PIECE].bitcast(FP8))
+            for start in range(first, cut, GROUP):
+                sorted_blocks.add((i, start))
+                nc.vector.tensor_scalar(
+                    out=x_wide[i][:, start : start + GROUP].rearrange("q (u p e) -> q p u e", u=2, e=2),
+                    in0=x_bytes[i][:, start : start + GROUP].bitcast(FP8).rearrange("q (p u e) -> q p u e", u=2, e=2),
+                    scalar1=ones[:],
+                    scalar2=None,
+                    op0=ALU.mult,
+                )
 
         def turn_x(n):
             i, g = divmod(n, GROUPS)
             x_turned[n] = psum_x.tile([P, 2, CHUNK], F32, name="x_turned")
             words = x_wide[i][:].bitcast(F32)
             for h in range(HALVES):
-                first = (h * K + g * GROUP) // 2
+                start = h * K + g * GROUP
+                first = start // 2
                 for u in range(2):
-                    nc.tensor.transpose(
-                        x_turned[n][:, u, h * P : (h + 1) * P], words[:, first + u : first + 2 * P : 2], ident[:]
-                    )
+                    if (i, start) in sorted_blocks:
+                        pairs = words[:, first + u * P : first + (u + 1) * P]
+                    else:
+                        pairs = words[:, first + u : first + 2 * P : 2]
+                    nc.tensor.transpose(x_turned[n][:, u, h * P : (h + 1) * P], pairs, ident[:])
 
         def raw_view(n):
             return x_turned[n][:].rearrange("p u s -> p (u s)").bitcast(BF16).rearrange("p (u s e) -> p s u e", u=2, e=2)
@@ -289,9 +301,9 @@ def tile_ricker_map_season_step_b5_kernel(tc, X_bytes, X_scale, A, r, gain, out_
         def live(n):
             return 0 <= n < STEPS
 
-        widen(0, PIECE)
+        widen(0, 2)
         widen(1, 0)
-        widen(2, PIECE)
+        widen(2, 2)
         for n in range(GROUPS):
             turn_x(n)
         group_a(0, 0, "S", 0)
@@ -356,7 +368,7 @@ def tile_ricker_map_season_step_b5_kernel(tc, X_bytes, X_scale, A, r, gain, out_
             if live(n - 2):
                 quantize_y(n - 2)
             if live(n + 6):
-                widen(n + 6, VECTOR_WIDEN)
+                widen(n + 6, n % 2)
             if live(n + 3):
                 quantize_x(n + 3)
             if live(n - 1):

@@ -24,16 +24,12 @@ CHUNK = 256
 HALVES = CHUNK // P
 CHUNKS = S // CHUNK
 STEPS = CHUNKS * GROUPS
+LAST = STEPS - 1
 PIECE = HALVES * K // GROUPS
-SCALAR_SITES = 0
-GPSIMD_SITES = 256
-Y_BUFS = 1
-HEAD_WIDEN = 0
-TAIL = ()
-TAIL2 = 23
-LANE = 23
-VECTOR_WIDEN = 0
-VECTOR_PLANES = ((0, 0, 4), (4, 4, 0), (0, 0, 4))
+QUADRANT = 32
+SCALE_ROWS = 4
+X_BANKS = 5
+RING_BANKS = 3
 
 
 def tile_ricker_map_season_step_b5_kernel(tc, X_bytes, X_scale, A, r, gain, out_0, out_1, out_2):
@@ -44,14 +40,16 @@ def tile_ricker_map_season_step_b5_kernel(tc, X_bytes, X_scale, A, r, gain, out_
     with ExitStack() as ctx:
         keep = ctx.enter_context(tc.tile_pool(name="keep", bufs=1))
         work = ctx.enter_context(tc.tile_pool(name="work", bufs=2))
-        psum_x = ctx.enter_context(tc.psum_pool(name="psum_x", bufs=5))
-        psum_s = ctx.enter_context(tc.psum_pool(name="psum_s", bufs=3))
+        psum_x = ctx.enter_context(tc.psum_pool(name="psum_x", bufs=X_BANKS))
+        psum_ring = ctx.enter_context(tc.psum_pool(name="psum_ring", bufs=RING_BANKS))
         ctx.enter_context(tc.manual_schedule())
 
+        zeros = keep.tile([P, 1], F32, name="zeros")
+        ones = keep.tile([P, 1], F32, name="ones")
+        nc.vector.memset(zeros[:], 0.0)
+        nc.scalar.activation(out=ones[:], in_=zeros[:], func=ACT.Exp)
         ident = keep.tile([P, P], F32, name="ident")
         make_identity(nc, ident[:])
-        warm = keep.tile([P, 1], F32, name="warm")
-        nc.scalar.activation(out=warm[:], in_=ident[:, 0:1], func=ACT.Exp)
 
         x_scale = keep.tile([P, GROUPS * PACK], F32, name="x_scale")
         r_bf = keep.tile([P, GROUPS * PACK], BF16, name="r_bf")
@@ -70,7 +68,7 @@ def tile_ricker_map_season_step_b5_kernel(tc, X_bytes, X_scale, A, r, gain, out_
                 a_scales[gk, gn] = keep.tile([P, GROUP], U8, name="a_scales_%d_%d" % (gk, gn), align_bytes=64)
         y_scales_first = keep.tile([P, S], U8, name="y_scales_first", align_bytes=64)
         y_scales_rest = keep.tile([P, S], U8, name="y_scales_rest", align_bytes=64)
-        y_scale_rows = [y_scales_first[:], y_scales_rest[:], y_scales_rest[4:P, :]]
+        y_scale_rows = [y_scales_first[:], y_scales_rest[:], y_scales_rest[SCALE_ROWS:P, :]]
 
         def load_species_vector(dst, src):
             nc.sync.dma_start(
@@ -90,7 +88,8 @@ def tile_ricker_map_season_step_b5_kernel(tc, X_bytes, X_scale, A, r, gain, out_
                 in_=A[gk * GROUP : (gk + 1) * GROUP, gn * GROUP : (gn + 1) * GROUP].rearrange("(p j) c -> p j c", j=PACK),
             )
 
-        load_x(0)
+        for h in range(HALVES):
+            nc.sync.dma_start(out=x_bytes[0][:, h * K : (h + 1) * K], in_=X_bytes[h * P : (h + 1) * P, :])
         load_species_vector(x_scale, X_scale)
         for gk in range(GROUPS):
             load_a(gk, 0)
@@ -103,40 +102,41 @@ def tile_ricker_map_season_step_b5_kernel(tc, X_bytes, X_scale, A, r, gain, out_
         for i in range(2, CHUNKS):
             load_x(i)
 
-
-        ones = keep.tile([P, 1], F32, name="ones")
-        nc.vector.memset(ones[:], 1.0)
-        sorted_blocks = set()
         x_wide = {}
+        sorted_spans = set()
         x_turned = {}
         x_grouped = {}
         x_codes = {}
         x_scales = {}
+        a_grouped = {}
         pressure = {}
         growth = {}
         y_planes = {}
         y_grouped = {}
         y_turned = {}
-        a_grouped = {}
         y_rows = {}
 
-        def widen(m, vector_blocks):
-            i, j = divmod(m, GROUPS)
-            if j == 0:
+        def widen_plain(i, start, stop):
+            nc.scalar.copy(out=x_wide[i][:, start:stop], in_=x_bytes[i][:, start:stop].bitcast(FP8))
+
+        def widen_sorted(i, start):
+            sorted_spans.add((i, start))
+            nc.vector.tensor_scalar(
+                out=x_wide[i][:, start : start + GROUP].rearrange("s (u p e) -> s p u e", u=2, e=2),
+                in0=x_bytes[i][:, start : start + GROUP].bitcast(FP8).rearrange("s (p u e) -> s p u e", u=2, e=2),
+                scalar1=ones[:],
+                scalar2=None,
+                op0=ALU.mult,
+            )
+
+        def widen(piece, vector_helps):
+            i, third = divmod(piece, GROUPS)
+            if third == 0:
                 x_wide[i] = work.tile([P, HALVES * K], BF16, name="x_wide")
-            first = j * PIECE
-            cut = first + vector_blocks * GROUP
-            if cut < first + PIECE:
-                nc.scalar.copy(out=x_wide[i][:, cut : first + PIECE], in_=x_bytes[i][:, cut : first + PIECE].bitcast(FP8))
-            for start in range(first, cut, GROUP):
-                sorted_blocks.add((i, start))
-                nc.vector.tensor_scalar(
-                    out=x_wide[i][:, start : start + GROUP].rearrange("q (u p e) -> q p u e", u=2, e=2),
-                    in0=x_bytes[i][:, start : start + GROUP].bitcast(FP8).rearrange("q (p u e) -> q p u e", u=2, e=2),
-                    scalar1=ones[:],
-                    scalar2=None,
-                    op0=ALU.mult,
-                )
+            start = third * PIECE
+            widen_plain(i, start + (GROUP if vector_helps else 0), start + PIECE)
+            if vector_helps:
+                widen_sorted(i, start)
 
         def turn_x(n):
             i, g = divmod(n, GROUPS)
@@ -144,15 +144,15 @@ def tile_ricker_map_season_step_b5_kernel(tc, X_bytes, X_scale, A, r, gain, out_
             words = x_wide[i][:].bitcast(F32)
             for h in range(HALVES):
                 start = h * K + g * GROUP
-                first = start // 2
+                word = start // 2
                 for u in range(2):
-                    if (i, start) in sorted_blocks:
-                        pairs = words[:, first + u * P : first + (u + 1) * P]
+                    if (i, start) in sorted_spans:
+                        pairs = words[:, word + u * P : word + (u + 1) * P]
                     else:
-                        pairs = words[:, first + u : first + 2 * P : 2]
+                        pairs = words[:, word + u : word + 2 * P : 2]
                     nc.tensor.transpose(x_turned[n][:, u, h * P : (h + 1) * P], pairs, ident[:])
 
-        def raw_view(n):
+        def byte_values(n):
             return x_turned[n][:].rearrange("p u s -> p (u s)").bitcast(BF16).rearrange("p (u s e) -> p s u e", u=2, e=2)
 
         def scale_x(n):
@@ -160,7 +160,7 @@ def tile_ricker_map_season_step_b5_kernel(tc, X_bytes, X_scale, A, r, gain, out_
             x_grouped[n] = work.tile([P, CHUNK * PACK], BF16, name="x_grouped", bufs=3, align_bytes=64)
             nc.vector.tensor_tensor(
                 out=x_grouped[n][:].rearrange("p (s u e) -> p s u e", u=2, e=2),
-                in0=raw_view(n),
+                in0=byte_values(n),
                 in1=x_scale[:, g * PACK : (g + 1) * PACK]
                 .rearrange("p (u e) -> p u e", u=2)
                 .unsqueeze(1)
@@ -173,43 +173,57 @@ def tile_ricker_map_season_step_b5_kernel(tc, X_bytes, X_scale, A, r, gain, out_
             x_scales[n] = work.tile([P, CHUNK], U8, name="x_scales", bufs=2 * GROUPS, align_bytes=64)
             nc.vector.quantize_mx(out=x_codes[n][:].bitcast(FP8X4), scales=x_scales[n][:], in_=x_grouped[n][:])
 
-        def group_a(gk, gn, engine, lane):
-            a_grouped[gk, gn] = work.tile([P, GROUP * PACK], BF16, name="a_grouped_%d" % lane, bufs=1, align_bytes=64)
-            src = a_raw[gk, gn][:].rearrange("p (j m t) -> p m t j", j=PACK, t=PACK)
+        def grouping_slot(slot, width, name):
+            return work.tile([P, width], BF16, name=name, tag="slot_%d" % slot, bufs=1, align_bytes=64)
+
+        def round_on_gpsimd(out, in_):
+            nc.gpsimd.tensor_scalar(out=out, in0=in_, scalar1=1.0, scalar2=1.0, op0=ALU.mult, op1=ALU.mult)
+
+        def a_views(gk, gn, slot):
+            a_grouped[gk, gn] = grouping_slot(slot, GROUP * PACK, "a_grouped")
             dst = a_grouped[gk, gn][:].rearrange("p (t m j) -> p m t j", t=PACK, j=PACK)
-            if engine == "G":
-                nc.gpsimd.tensor_scalar(out=dst.rearrange("p m t j -> p t m j"), in0=src.rearrange("p m t j -> p t m j"), scalar1=1.0, scalar2=1.0, op0=ALU.mult, op1=ALU.mult)
-            elif engine == "S":
-                nc.scalar.copy(out=dst, in_=src)
-            elif engine == "V":
-                nc.vector.tensor_copy(out=dst, in_=src)
-            else:
-                nc.scalar.copy(out=dst[:, :, 2:, :], in_=src[:, :, 2:, :])
-                nc.vector.tensor_copy(out=dst[:, :, :2, :], in_=src[:, :, :2, :])
+            src = a_raw[gk, gn][:].rearrange("p (j m t) -> p m t j", j=PACK, t=PACK)
+            return dst, src
+
+        def group_a_on_vector(gk, gn, slot):
+            dst, src = a_views(gk, gn, slot)
+            nc.vector.tensor_copy(out=dst, in_=src)
+
+        def group_a_on_scalar(gk, gn, slot):
+            dst, src = a_views(gk, gn, slot)
+            nc.scalar.copy(out=dst, in_=src)
+
+        def group_a_on_both(gk, gn, slot):
+            dst, src = a_views(gk, gn, slot)
+            nc.scalar.copy(out=dst[:, :, 2:, :], in_=src[:, :, 2:, :])
+            nc.vector.tensor_copy(out=dst[:, :, :2, :], in_=src[:, :, :2, :])
+
+        def group_a_on_gpsimd(gk, gn, slot):
+            dst, src = a_views(gk, gn, slot)
+            round_on_gpsimd(dst.rearrange("p m t j -> p t m j"), src.rearrange("p m t j -> p t m j"))
 
         def quantize_a(gk, gn):
             nc.vector.quantize_mx(out=a_codes[gk, gn][:].bitcast(FP8X4), scales=a_scales[gk, gn][:], in_=a_grouped[gk, gn][:])
 
-        def multiply(n, halves):
+        def multiply(n, u):
             i, gn = divmod(n, GROUPS)
-            for u in halves:
-                pressure[n, u] = psum_s.tile([P, 2, CHUNK], F32, name="pressure", tag="bank")
-                for e in range(2):
-                    cols = slice((2 * u + e) * P, (2 * u + e + 1) * P)
-                    for gk in range(GROUPS):
-                        nc.tensor.matmul_mx(
-                            out=pressure[n, u][:, e, :],
-                            lhsT=a_codes[gk, gn][:, cols].bitcast(FP8X4),
-                            lhsT_scale=a_scales[gk, gn][:, cols],
-                            rhs=x_codes[i * GROUPS + gk][:].bitcast(FP8X4),
-                            rhs_scale=x_scales[i * GROUPS + gk][:],
-                            start=(gk == 0),
-                            stop=(gk == GROUPS - 1),
-                        )
+            pressure[n, u] = psum_ring.tile([P, 2, CHUNK], F32, name="pressure", tag="bank")
+            for e in range(2):
+                cols = slice((2 * u + e) * P, (2 * u + e + 1) * P)
+                for gk in range(GROUPS):
+                    nc.tensor.matmul_mx(
+                        out=pressure[n, u][:, e, :],
+                        lhsT=a_codes[gk, gn][:, cols].bitcast(FP8X4),
+                        lhsT_scale=a_scales[gk, gn][:, cols],
+                        rhs=x_codes[i * GROUPS + gk][:].bitcast(FP8X4),
+                        rhs_scale=x_scales[i * GROUPS + gk][:],
+                        start=(gk == 0),
+                        stop=(gk == GROUPS - 1),
+                    )
 
-        def exponentiate(n, u):
+        def exponentiate(n):
             g = n % GROUPS
-            for t in (2 * u, 2 * u + 1):
+            for t in range(PACK):
                 growth[n, t] = work.tile([P, CHUNK], F32, name="growth", bufs=3 * PACK)
                 col = g * PACK + t
                 nc.scalar.activation(
@@ -223,12 +237,12 @@ def tile_ricker_map_season_step_b5_kernel(tc, X_bytes, X_scale, A, r, gain, out_
         def grow(n):
             g = n % GROUPS
             y_planes[n] = work.tile([P, PACK * CHUNK], F32, name="y_planes", bufs=3)
-            raw = raw_view(n)
+            values = byte_values(n)
             for t in range(PACK):
                 col = g * PACK + t
                 nc.vector.scalar_tensor_tensor(
                     out=y_planes[n][:, t * CHUNK : (t + 1) * CHUNK],
-                    in0=raw[:, :, t // 2, t % 2],
+                    in0=values[:, :, t // 2, t % 2],
                     scalar=factor[:, col : col + 1],
                     in1=growth[n, t][:],
                     op0=ALU.mult,
@@ -236,26 +250,27 @@ def tile_ricker_map_season_step_b5_kernel(tc, X_bytes, X_scale, A, r, gain, out_
                 )
 
         def group_y(n):
-            y_grouped[n] = work.tile([P, CHUNK * PACK], BF16, name="y_grouped", tag="a_grouped_%d" % (0 if n == LANE else 1), bufs=1, align_bytes=64)
-            src = y_planes[n][:].rearrange("p (t c i) -> p c t i", t=PACK, i=4)
-            dst = y_grouped[n][:].rearrange("p (c i t) -> p c t i", t=PACK, i=4)
-            cut = SCALAR_SITES // 4
-            cut2 = cut + GPSIMD_SITES // 4
-            if n >= TAIL2:
-                cut, cut2 = 0, 0
-            if cut:
-                nc.scalar.copy(out=dst[:, :cut], in_=src[:, :cut])
-            if cut2 > cut:
-                nc.gpsimd.tensor_scalar(
-                    out=y_grouped[n][:].rearrange("p (s t) -> p s t", t=PACK)[:, 4 * cut : 4 * cut2],
-                    in0=y_planes[n][:].rearrange("p (t s) -> p s t", t=PACK)[:, 4 * cut : 4 * cut2],
-                    scalar1=1.0,
-                    scalar2=1.0,
-                    op0=ALU.mult,
-                    op1=ALU.mult,
+            y_grouped[n] = grouping_slot(1, CHUNK * PACK, "y_grouped")
+            round_on_gpsimd(
+                y_grouped[n][:].rearrange("p (s t) -> p s t", t=PACK),
+                y_planes[n][:].rearrange("p (t s) -> p s t", t=PACK),
+            )
+
+        def group_last_y():
+            y_grouped[LAST] = grouping_slot(0, CHUNK * PACK, "y_grouped")
+            nc.vector.tensor_copy(
+                out=y_grouped[LAST][:].rearrange("p (w v t) -> p w t v", t=PACK, v=4),
+                in_=y_planes[LAST][:].rearrange("p (t w v) -> p w t v", t=PACK, v=4),
+            )
+
+        def store_y_scales(tile, groups, sites):
+            cols = slice(sites.start // 4, sites.stop // 4)
+            rows = SCALE_ROWS * (groups.stop - groups.start)
+            for q in range(P // QUADRANT):
+                nc.sync.dma_start(
+                    out=scales_out[groups, SCALE_ROWS * q : SCALE_ROWS * (q + 1), cols],
+                    in_=tile[:].bitcast(I32)[QUADRANT * q : QUADRANT * q + rows, cols],
                 )
-            if cut2 < CHUNK // 4:
-                nc.vector.tensor_copy(out=dst[:, cut2:], in_=src[:, cut2:])
 
         def quantize_y(n):
             i, g = divmod(n, GROUPS)
@@ -263,137 +278,124 @@ def tile_ricker_map_season_step_b5_kernel(tc, X_bytes, X_scale, A, r, gain, out_
             y_codes = work.tile([P, CHUNK], U32, name="y_codes", bufs=4, align_bytes=64)
             nc.vector.quantize_mx(out=y_codes[:].bitcast(FP8X4), scales=y_scale_rows[g][:, sites], in_=y_grouped[n][:])
             nc.sync.dma_start(out=words_out[g][:, sites], in_=y_codes[:].bitcast(I32))
-            if (i + 1) % (CHUNKS // 2) == 0 and g != 1:
-                cols = slice((i + 1) * CHUNK // 4 - S // 8, (i + 1) * CHUNK // 4)
-                groups = slice(0, 1) if g == 0 else slice(1, GROUPS)
-                rows = 4 * (groups.stop - groups.start)
-                tile = y_scales_first if g == 0 else y_scales_rest
-                for q in range(4):
-                    nc.sync.dma_start(
-                        out=scales_out[groups, 4 * q : 4 * q + 4, cols],
-                        in_=tile[:].bitcast(I32)[32 * q : 32 * q + rows, cols],
-                    )
+            if sites.stop % (S // 2) == 0:
+                done = slice(sites.stop - S // 2, sites.stop)
+                if g == 0:
+                    store_y_scales(y_scales_first, slice(0, 1), done)
+                if g == GROUPS - 1:
+                    store_y_scales(y_scales_rest, slice(1, GROUPS), done)
 
-        def turn_y(n, h):
-            if h == 0 and n >= STEPS - 5:
-                y_turned[n, h] = psum_x.tile([P, PACK, P], F32, name="y_turned", tag="x_turned")
-            else:
-                y_turned[n, h] = psum_s.tile([P, PACK, P], F32, name="y_turned", tag="bank")
-            if True:
+        def turn_y(n):
+            for h in range(HALVES):
+                if h == 0 and n + X_BANKS >= STEPS:
+                    y_turned[n, h] = psum_x.tile([P, PACK, P], F32, name="y_turned", tag="x_turned")
+                else:
+                    y_turned[n, h] = psum_ring.tile([P, PACK, P], F32, name="y_turned", tag="bank")
                 for t in range(PACK):
                     first = t * CHUNK + h * P
                     nc.tensor.transpose(y_turned[n, h][:, t, :], y_planes[n][:, first : first + P], ident[:])
 
         def copy_y(n, h):
-            copy = nc.vector.tensor_copy if h == 1 and n in TAIL else nc.scalar.copy
             if h == 0:
                 y_rows[n] = work.tile([P, HALVES, GROUP], F32, name="y_rows", bufs=3)
-            copy(
+            nc.scalar.copy(
                 out=y_rows[n][:, h, :].rearrange("s (p t) -> s p t", t=PACK),
                 in_=y_turned[n, h][:].rearrange("s t p -> s p t"),
             )
 
-        def store_y(n, halves):
+        def store_y(n):
             i, g = divmod(n, GROUPS)
-            rows = out_0[i * CHUNK : (i + 1) * CHUNK, g * GROUP : (g + 1) * GROUP].rearrange("(h s) c -> s h c", s=P)
-            nc.sync.dma_start(out=rows[:, halves, :], in_=y_rows[n][:, halves, :])
+            nc.sync.dma_start(
+                out=out_0[i * CHUNK : (i + 1) * CHUNK, g * GROUP : (g + 1) * GROUP].rearrange("(h s) c -> s h c", s=P),
+                in_=y_rows[n][:],
+            )
 
-        def live(n):
-            return 0 <= n < STEPS
+        def store_and_multiply(leaving, coming):
+            copy_y(leaving, 0)
+            if coming < STEPS:
+                multiply(coming, 0)
+            copy_y(leaving, 1)
+            store_y(leaving)
+            if coming < STEPS:
+                multiply(coming, 1)
 
-        widen(0, 2)
-        widen(1, 0)
-        widen(2, 2)
-        for n in range(GROUPS):
-            turn_x(n)
-        group_a(0, 0, "S", 0)
-        group_a(1, 0, "G", 1)
-        group_a(2, 0, "S", 2)
-        for n in range(GROUPS):
-            scale_x(n)
+        x_wide[0] = work.tile([P, HALVES * K], BF16, name="x_wide")
+        for g in range(GROUPS):
+            widen_sorted(0, g * GROUP)
+            widen_plain(0, K + g * GROUP, K + (g + 1) * GROUP)
+            turn_x(g)
+        group_a_on_gpsimd(0, 0, slot=0)
+        group_a_on_scalar(1, 0, slot=1)
+        for g in range(GROUPS):
+            scale_x(g)
+        quantize_x(0)
+        quantize_a(0, 0)
+        quantize_x(1)
+        group_a_on_both(2, 0, slot=2)
+        quantize_x(2)
+        quantize_a(1, 0)
+        quantize_a(2, 0)
         nc.vector.tensor_copy(out=rate[:], in_=r_bf[:])
         nc.vector.tensor_tensor(out=factor[:], in0=x_scale[:], in1=gain_bf[:], op=ALU.mult)
-        for n in range(GROUPS):
-            quantize_x(n)
-            quantize_a(n, 0)
-        widen(3, HEAD_WIDEN)
-        widen(4, HEAD_WIDEN)
-        widen(5, HEAD_WIDEN)
-        multiply(0, (0, 1))
+
+        for third in range(GROUPS):
+            widen(GROUPS + third, False)
+        multiply(0, 0)
+        multiply(0, 1)
         turn_x(3)
         turn_x(4)
-        group_a(0, 1, "V", 0)
-        group_a(2, 1, "S", 1)
-        exponentiate(0, 0)
-        exponentiate(0, 1)
+        group_a_on_vector(0, 1, slot=0)
+        group_a_on_scalar(2, 1, slot=1)
+        exponentiate(0)
         quantize_a(0, 1)
-        group_a(1, 1, "G", 0)
+        group_a_on_gpsimd(1, 1, slot=0)
         scale_x(3)
         grow(0)
         scale_x(4)
-        turn_y(0, 0)
-        turn_y(0, 1)
+        turn_y(0)
         turn_x(5)
         quantize_a(1, 1)
         quantize_a(2, 1)
-        group_a(1, 2, "S", 2)
-        copy_y(0, 0)
-        multiply(1, (0,))
-        copy_y(0, 1)
-        store_y(0, slice(0, 2))
-        multiply(1, (1,))
+
+        group_a_on_scalar(1, 2, slot=2)
+        store_and_multiply(0, 1)
         quantize_x(3)
-        group_a(0, 2, "V", 0)
+        group_a_on_vector(0, 2, slot=0)
         quantize_x(4)
-        group_a(2, 2, "VS", 1)
-        exponentiate(1, 0)
-        exponentiate(1, 1)
-        quantize_a(0, 2)
-        quantize_a(1, 2)
-        quantize_a(2, 2)
-        widen(6, 0)
-        widen(7, 0)
-        multiply(2, (0, 1))
+        group_a_on_both(2, 2, slot=1)
+        exponentiate(1)
+        for gk in range(GROUPS):
+            quantize_a(gk, 2)
+        widen(2 * GROUPS, False)
+        widen(2 * GROUPS + 1, False)
+        multiply(2, 0)
+        multiply(2, 1)
         group_y(0)
         grow(1)
         scale_x(5)
-        exponentiate(2, 0)
-        exponentiate(2, 1)
+        exponentiate(2)
+
         for n in range(2, STEPS):
-            if live(n + 4):
+            if n + 4 < STEPS:
                 turn_x(n + 4)
-            if live(n - 1):
-                turn_y(n - 1, 0)
-                turn_y(n - 1, 1)
-            if live(n - 2):
-                quantize_y(n - 2)
-            if live(n + 6):
-                widen(n + 6, n % 2)
-            if live(n + 3):
+            turn_y(n - 1)
+            quantize_y(n - 2)
+            if n + 6 < STEPS:
+                widen(n + 6, n % 2 == 1)
+            if n + 3 < STEPS:
                 quantize_x(n + 3)
-            if live(n - 1):
-                group_y(n - 1)
-            if live(n - 1):
-                copy_y(n - 1, 0)
-            if live(n + 1):
-                multiply(n + 1, (0,))
-            if live(n - 1):
-                copy_y(n - 1, 1)
-                store_y(n - 1, slice(0, 2))
-            if live(n + 1):
-                multiply(n + 1, (1,))
-                exponentiate(n + 1, 0)
-                exponentiate(n + 1, 1)
-            if live(n):
-                grow(n)
-            if live(n + 4):
+            group_y(n - 1)
+            store_and_multiply(n - 1, n + 1)
+            if n < LAST:
+                exponentiate(n + 1)
+            grow(n)
+            if n + 4 < STEPS:
                 scale_x(n + 4)
-        last = STEPS - 1
-        turn_y(last, 0)
-        turn_y(last, 1)
-        group_y(last)
-        quantize_y(last - 1)
-        copy_y(last, 0)
-        copy_y(last, 1)
-        store_y(last, slice(0, 2))
-        quantize_y(last)
+
+        turn_y(LAST)
+        group_last_y()
+        quantize_y(LAST - 1)
+        for h in range(HALVES):
+            copy_y(LAST, h)
+        store_y(LAST)
+        quantize_y(LAST)

from contextlib import ExitStack

import concourse.mybir as mybir
from concourse.masks import make_identity

S, K = 2048, 1536
FLOPS = 2 * S * K * K

F32 = mybir.dt.float32
BF16 = mybir.dt.bfloat16
I32 = mybir.dt.int32
U32 = mybir.dt.uint32
U8 = mybir.dt.uint8
FP8 = mybir.dt.float8_e4m3fn
FP8X4 = mybir.dt.float8_e4m3fn_x4
ALU = mybir.AluOpType
ACT = mybir.ActivationFunctionType

P = 128
PACK = 4
GROUP = P * PACK
GROUPS = K // GROUP
CHUNK = 256
HALVES = CHUNK // P
CHUNKS = S // CHUNK
STEPS = CHUNKS * GROUPS
LAST = STEPS - 1
PIECE = HALVES * K // GROUPS
QUADRANT = 32
SCALE_ROWS = 4
X_BANKS = 5
RING_BANKS = 3


def tile_ricker_map_season_step_b5_kernel(tc, X_bytes, X_scale, A, r, gain, out_0, out_1, out_2):
    nc = tc.nc
    words_out = out_1.rearrange("g p m t -> g p (m t)").bitcast(I32)
    scales_out = out_2.bitcast(I32)

    with ExitStack() as ctx:
        keep = ctx.enter_context(tc.tile_pool(name="keep", bufs=1))
        work = ctx.enter_context(tc.tile_pool(name="work", bufs=2))
        psum_x = ctx.enter_context(tc.psum_pool(name="psum_x", bufs=X_BANKS))
        psum_ring = ctx.enter_context(tc.psum_pool(name="psum_ring", bufs=RING_BANKS))
        ctx.enter_context(tc.manual_schedule())

        zeros = keep.tile([P, 1], F32, name="zeros")
        ones = keep.tile([P, 1], F32, name="ones")
        nc.vector.memset(zeros[:], 0.0)
        nc.scalar.activation(out=ones[:], in_=zeros[:], func=ACT.Exp)
        ident = keep.tile([P, P], F32, name="ident")
        make_identity(nc, ident[:])

        x_scale = keep.tile([P, GROUPS * PACK], F32, name="x_scale")
        r_bf = keep.tile([P, GROUPS * PACK], BF16, name="r_bf")
        gain_bf = keep.tile([P, GROUPS * PACK], BF16, name="gain_bf")
        rate = keep.tile([P, GROUPS * PACK], F32, name="rate")
        factor = keep.tile([P, GROUPS * PACK], F32, name="factor")

        x_bytes = [keep.tile([P, HALVES * K], U8, name="x_bytes_%d" % i) for i in range(CHUNKS)]
        a_raw = {}
        a_codes = {}
        a_scales = {}
        for gn in range(GROUPS):
            for gk in range(GROUPS):
                a_raw[gk, gn] = keep.tile([P, PACK * GROUP], BF16, name="a_raw_%d_%d" % (gk, gn))
                a_codes[gk, gn] = keep.tile([P, GROUP], U32, name="a_codes_%d_%d" % (gk, gn), align_bytes=64)
                a_scales[gk, gn] = keep.tile([P, GROUP], U8, name="a_scales_%d_%d" % (gk, gn), align_bytes=64)
        y_scales_first = keep.tile([P, S], U8, name="y_scales_first", align_bytes=64)
        y_scales_rest = keep.tile([P, S], U8, name="y_scales_rest", align_bytes=64)
        y_scale_rows = [y_scales_first[:], y_scales_rest[:], y_scales_rest[SCALE_ROWS:P, :]]

        def load_species_vector(dst, src):
            nc.sync.dma_start(
                out=dst[:].rearrange("p (g t) -> p g t", t=PACK),
                in_=src.rearrange("o (g p t) -> p (o g) t", p=P, t=PACK),
            )

        def load_x(i):
            nc.sync.dma_start(
                out=x_bytes[i][:].rearrange("p (h k) -> p h k", h=HALVES),
                in_=X_bytes[i * CHUNK : (i + 1) * CHUNK, :].rearrange("(h p) k -> p h k", p=P),
            )

        def load_a(gk, gn):
            nc.sync.dma_start(
                out=a_raw[gk, gn][:].rearrange("p (j c) -> p j c", j=PACK),
                in_=A[gk * GROUP : (gk + 1) * GROUP, gn * GROUP : (gn + 1) * GROUP].rearrange("(p j) c -> p j c", j=PACK),
            )

        for h in range(HALVES):
            nc.sync.dma_start(out=x_bytes[0][:, h * K : (h + 1) * K], in_=X_bytes[h * P : (h + 1) * P, :])
        load_species_vector(x_scale, X_scale)
        for gk in range(GROUPS):
            load_a(gk, 0)
        load_x(1)
        load_species_vector(r_bf, r)
        load_species_vector(gain_bf, gain)
        for gn in range(1, GROUPS):
            for gk in range(GROUPS):
                load_a(gk, gn)
        for i in range(2, CHUNKS):
            load_x(i)

        x_wide = {}
        sorted_spans = set()
        x_turned = {}
        x_grouped = {}
        x_codes = {}
        x_scales = {}
        a_grouped = {}
        pressure = {}
        growth = {}
        y_planes = {}
        y_grouped = {}
        y_turned = {}
        y_rows = {}

        def widen_plain(i, start, stop):
            nc.scalar.copy(out=x_wide[i][:, start:stop], in_=x_bytes[i][:, start:stop].bitcast(FP8))

        def widen_sorted(i, start):
            sorted_spans.add((i, start))
            nc.vector.tensor_scalar(
                out=x_wide[i][:, start : start + GROUP].rearrange("s (u p e) -> s p u e", u=2, e=2),
                in0=x_bytes[i][:, start : start + GROUP].bitcast(FP8).rearrange("s (p u e) -> s p u e", u=2, e=2),
                scalar1=ones[:],
                scalar2=None,
                op0=ALU.mult,
            )

        def widen(piece, vector_helps):
            i, third = divmod(piece, GROUPS)
            if third == 0:
                x_wide[i] = work.tile([P, HALVES * K], BF16, name="x_wide")
            start = third * PIECE
            widen_plain(i, start + (GROUP if vector_helps else 0), start + PIECE)
            if vector_helps:
                widen_sorted(i, start)

        def turn_x(n):
            i, g = divmod(n, GROUPS)
            x_turned[n] = psum_x.tile([P, 2, CHUNK], F32, name="x_turned")
            words = x_wide[i][:].bitcast(F32)
            for h in range(HALVES):
                start = h * K + g * GROUP
                word = start // 2
                for u in range(2):
                    if (i, start) in sorted_spans:
                        pairs = words[:, word + u * P : word + (u + 1) * P]
                    else:
                        pairs = words[:, word + u : word + 2 * P : 2]
                    nc.tensor.transpose(x_turned[n][:, u, h * P : (h + 1) * P], pairs, ident[:])

        def byte_values(n):
            return x_turned[n][:].rearrange("p u s -> p (u s)").bitcast(BF16).rearrange("p (u s e) -> p s u e", u=2, e=2)

        def scale_x(n):
            g = n % GROUPS
            x_grouped[n] = work.tile([P, CHUNK * PACK], BF16, name="x_grouped", bufs=3, align_bytes=64)
            nc.vector.tensor_tensor(
                out=x_grouped[n][:].rearrange("p (s u e) -> p s u e", u=2, e=2),
                in0=byte_values(n),
                in1=x_scale[:, g * PACK : (g + 1) * PACK]
                .rearrange("p (u e) -> p u e", u=2)
                .unsqueeze(1)
                .to_broadcast([P, CHUNK, 2, 2]),
                op=ALU.mult,
            )

        def quantize_x(n):
            x_codes[n] = work.tile([P, CHUNK], U32, name="x_codes", bufs=2 * GROUPS, align_bytes=64)
            x_scales[n] = work.tile([P, CHUNK], U8, name="x_scales", bufs=2 * GROUPS, align_bytes=64)
            nc.vector.quantize_mx(out=x_codes[n][:].bitcast(FP8X4), scales=x_scales[n][:], in_=x_grouped[n][:])

        def grouping_slot(slot, width, name):
            return work.tile([P, width], BF16, name=name, tag="slot_%d" % slot, bufs=1, align_bytes=64)

        def round_on_gpsimd(out, in_):
            nc.gpsimd.tensor_scalar(out=out, in0=in_, scalar1=1.0, scalar2=1.0, op0=ALU.mult, op1=ALU.mult)

        def a_views(gk, gn, slot):
            a_grouped[gk, gn] = grouping_slot(slot, GROUP * PACK, "a_grouped")
            dst = a_grouped[gk, gn][:].rearrange("p (t m j) -> p m t j", t=PACK, j=PACK)
            src = a_raw[gk, gn][:].rearrange("p (j m t) -> p m t j", j=PACK, t=PACK)
            return dst, src

        def group_a_on_vector(gk, gn, slot):
            dst, src = a_views(gk, gn, slot)
            nc.vector.tensor_copy(out=dst, in_=src)

        def group_a_on_scalar(gk, gn, slot):
            dst, src = a_views(gk, gn, slot)
            nc.scalar.copy(out=dst, in_=src)

        def group_a_on_both(gk, gn, slot):
            dst, src = a_views(gk, gn, slot)
            nc.scalar.copy(out=dst[:, :, 2:, :], in_=src[:, :, 2:, :])
            nc.vector.tensor_copy(out=dst[:, :, :2, :], in_=src[:, :, :2, :])

        def group_a_on_gpsimd(gk, gn, slot):
            dst, src = a_views(gk, gn, slot)
            round_on_gpsimd(dst.rearrange("p m t j -> p t m j"), src.rearrange("p m t j -> p t m j"))

        def quantize_a(gk, gn):
            nc.vector.quantize_mx(out=a_codes[gk, gn][:].bitcast(FP8X4), scales=a_scales[gk, gn][:], in_=a_grouped[gk, gn][:])

        def multiply(n, u):
            i, gn = divmod(n, GROUPS)
            pressure[n, u] = psum_ring.tile([P, 2, CHUNK], F32, name="pressure", tag="bank")
            for e in range(2):
                cols = slice((2 * u + e) * P, (2 * u + e + 1) * P)
                for gk in range(GROUPS):
                    nc.tensor.matmul_mx(
                        out=pressure[n, u][:, e, :],
                        lhsT=a_codes[gk, gn][:, cols].bitcast(FP8X4),
                        lhsT_scale=a_scales[gk, gn][:, cols],
                        rhs=x_codes[i * GROUPS + gk][:].bitcast(FP8X4),
                        rhs_scale=x_scales[i * GROUPS + gk][:],
                        start=(gk == 0),
                        stop=(gk == GROUPS - 1),
                    )

        def exponentiate(n):
            g = n % GROUPS
            for t in range(PACK):
                growth[n, t] = work.tile([P, CHUNK], F32, name="growth", bufs=3 * PACK)
                col = g * PACK + t
                nc.scalar.activation(
                    out=growth[n, t][:],
                    in_=pressure[n, t // 2][:, t % 2, :],
                    func=ACT.Exp,
                    bias=rate[:, col : col + 1],
                    scale=-1.0,
                )

        def grow(n):
            g = n % GROUPS
            y_planes[n] = work.tile([P, PACK * CHUNK], F32, name="y_planes", bufs=3)
            values = byte_values(n)
            for t in range(PACK):
                col = g * PACK + t
                nc.vector.scalar_tensor_tensor(
                    out=y_planes[n][:, t * CHUNK : (t + 1) * CHUNK],
                    in0=values[:, :, t // 2, t % 2],
                    scalar=factor[:, col : col + 1],
                    in1=growth[n, t][:],
                    op0=ALU.mult,
                    op1=ALU.mult,
                )

        def group_y(n):
            y_grouped[n] = grouping_slot(1, CHUNK * PACK, "y_grouped")
            round_on_gpsimd(
                y_grouped[n][:].rearrange("p (s t) -> p s t", t=PACK),
                y_planes[n][:].rearrange("p (t s) -> p s t", t=PACK),
            )

        def group_last_y():
            y_grouped[LAST] = grouping_slot(0, CHUNK * PACK, "y_grouped")
            nc.vector.tensor_copy(
                out=y_grouped[LAST][:].rearrange("p (w v t) -> p w t v", t=PACK, v=4),
                in_=y_planes[LAST][:].rearrange("p (t w v) -> p w t v", t=PACK, v=4),
            )

        def store_y_scales(tile, groups, sites):
            cols = slice(sites.start // 4, sites.stop // 4)
            rows = SCALE_ROWS * (groups.stop - groups.start)
            for q in range(P // QUADRANT):
                nc.sync.dma_start(
                    out=scales_out[groups, SCALE_ROWS * q : SCALE_ROWS * (q + 1), cols],
                    in_=tile[:].bitcast(I32)[QUADRANT * q : QUADRANT * q + rows, cols],
                )

        def quantize_y(n):
            i, g = divmod(n, GROUPS)
            sites = slice(i * CHUNK, (i + 1) * CHUNK)
            y_codes = work.tile([P, CHUNK], U32, name="y_codes", bufs=4, align_bytes=64)
            nc.vector.quantize_mx(out=y_codes[:].bitcast(FP8X4), scales=y_scale_rows[g][:, sites], in_=y_grouped[n][:])
            nc.sync.dma_start(out=words_out[g][:, sites], in_=y_codes[:].bitcast(I32))
            if sites.stop % (S // 2) == 0:
                done = slice(sites.stop - S // 2, sites.stop)
                if g == 0:
                    store_y_scales(y_scales_first, slice(0, 1), done)
                if g == GROUPS - 1:
                    store_y_scales(y_scales_rest, slice(1, GROUPS), done)

        def turn_y(n):
            for h in range(HALVES):
                if h == 0 and n + X_BANKS >= STEPS:
                    y_turned[n, h] = psum_x.tile([P, PACK, P], F32, name="y_turned", tag="x_turned")
                else:
                    y_turned[n, h] = psum_ring.tile([P, PACK, P], F32, name="y_turned", tag="bank")
                for t in range(PACK):
                    first = t * CHUNK + h * P
                    nc.tensor.transpose(y_turned[n, h][:, t, :], y_planes[n][:, first : first + P], ident[:])

        def copy_y(n, h):
            if h == 0:
                y_rows[n] = work.tile([P, HALVES, GROUP], F32, name="y_rows", bufs=3)
            nc.scalar.copy(
                out=y_rows[n][:, h, :].rearrange("s (p t) -> s p t", t=PACK),
                in_=y_turned[n, h][:].rearrange("s t p -> s p t"),
            )

        def store_y(n):
            i, g = divmod(n, GROUPS)
            nc.sync.dma_start(
                out=out_0[i * CHUNK : (i + 1) * CHUNK, g * GROUP : (g + 1) * GROUP].rearrange("(h s) c -> s h c", s=P),
                in_=y_rows[n][:],
            )

        def store_and_multiply(leaving, coming):
            copy_y(leaving, 0)
            if coming < STEPS:
                multiply(coming, 0)
            copy_y(leaving, 1)
            store_y(leaving)
            if coming < STEPS:
                multiply(coming, 1)

        x_wide[0] = work.tile([P, HALVES * K], BF16, name="x_wide")
        for g in range(GROUPS):
            widen_sorted(0, g * GROUP)
            widen_plain(0, K + g * GROUP, K + (g + 1) * GROUP)
            turn_x(g)
        group_a_on_gpsimd(0, 0, slot=0)
        group_a_on_scalar(1, 0, slot=1)
        for g in range(GROUPS):
            scale_x(g)
        quantize_x(0)
        quantize_a(0, 0)
        quantize_x(1)
        group_a_on_both(2, 0, slot=2)
        quantize_x(2)
        quantize_a(1, 0)
        quantize_a(2, 0)
        nc.vector.tensor_copy(out=rate[:], in_=r_bf[:])
        nc.vector.tensor_tensor(out=factor[:], in0=x_scale[:], in1=gain_bf[:], op=ALU.mult)

        for third in range(GROUPS):
            widen(GROUPS + third, False)
        multiply(0, 0)
        multiply(0, 1)
        turn_x(3)
        turn_x(4)
        group_a_on_vector(0, 1, slot=0)
        group_a_on_scalar(2, 1, slot=1)
        exponentiate(0)
        quantize_a(0, 1)
        group_a_on_gpsimd(1, 1, slot=0)
        scale_x(3)
        grow(0)
        scale_x(4)
        turn_y(0)
        turn_x(5)
        quantize_a(1, 1)
        quantize_a(2, 1)

        group_a_on_scalar(1, 2, slot=2)
        store_and_multiply(0, 1)
        quantize_x(3)
        group_a_on_vector(0, 2, slot=0)
        quantize_x(4)
        group_a_on_both(2, 2, slot=1)
        exponentiate(1)
        for gk in range(GROUPS):
            quantize_a(gk, 2)
        widen(2 * GROUPS, False)
        widen(2 * GROUPS + 1, False)
        multiply(2, 0)
        multiply(2, 1)
        group_y(0)
        grow(1)
        scale_x(5)
        exponentiate(2)

        for n in range(2, STEPS):
            if n + 4 < STEPS:
                turn_x(n + 4)
            turn_y(n - 1)
            quantize_y(n - 2)
            if n + 6 < STEPS:
                widen(n + 6, n % 2 == 1)
            if n + 3 < STEPS:
                quantize_x(n + 3)
            group_y(n - 1)
            store_and_multiply(n - 1, n + 1)
            if n < LAST:
                exponentiate(n + 1)
            grow(n)
            if n + 4 < STEPS:
                scale_x(n + 4)

        turn_y(LAST)
        group_last_y()
        quantize_y(LAST - 1)
        for h in range(HALVES):
            copy_y(LAST, h)
        store_y(LAST)
        quantize_y(LAST)
